import numpy as np
import ml_dtypes


def mxq(x, axis, fmt="e4m3"):
    dtype, down = {"e4m3": (ml_dtypes.float8_e4m3fn, 7), "e5m2": (ml_dtypes.float8_e5m2, 14)}[fmt]
    v = np.moveaxis(np.asarray(x, np.float32).astype(ml_dtypes.bfloat16).astype(np.float64), axis, -1)
    blocks = v.reshape(v.shape[:-1] + (-1, 32))
    amax = np.abs(blocks).max(-1, keepdims=True)
    byte = np.maximum(np.where(amax > 0, np.frexp(amax)[1] - 1 + 127, 0) - down, 1)
    scale = np.exp2(byte - 127.0)
    codes = (blocks / scale).astype(np.float32).astype(dtype).astype(np.float64)
    return np.moveaxis((codes * scale).reshape(v.shape), -1, axis)


WIDE = False


def mx_kscale(k):
    if not WIDE:
        return np.ones(k)
    levels = np.array([10, -10, 5, -5, 0])
    if k % 512:
        return np.exp2(np.random.permutation(np.resize(levels, k // 32))).repeat(32)
    a = np.empty((k // 512, 16))
    for p in range(k // 512):
        a[p, :8] = np.random.permutation(np.resize(levels, 8))
        for g in range(8):
            far = levels[np.abs(levels - a[p, g]) >= 10]
            a[p, g + 8] = far[np.random.randint(len(far))]
    return np.exp2(a.ravel()).repeat(32)


def f64(x):
    return np.asarray(x).astype(np.float64)


def striped(idx):
    return np.tile(idx.reshape(-1, 16).T, (8, 1)).astype(np.uint16)


def unstriped(offs):
    return offs[:16].T.reshape(-1).astype(np.int64)


E2M1 = np.array([0.0, 0.5, 1.0, 1.5, 2.0, 3.0, 4.0, 6.0, -0.0, -0.5, -1.0, -1.5, -2.0, -3.0, -4.0, -6.0])


def pack_weight(w, fmt):
    k, n = w.shape
    w = f64(np.asarray(w, np.float32).astype(ml_dtypes.bfloat16)).reshape(k // 32, 32, n)
    amax = np.abs(w).max(1)
    if fmt == "e4m3":
        byte = np.frexp(amax)[1] - 1 + 127 - 7
    else:
        mant, ex = np.frexp(amax / 6.0)
        byte = np.where(mant > 0.5, ex, ex - 1) + 127
    byte = np.clip(np.where(amax > 0, byte, 1), 1, 254)
    scaled = (w * np.exp2(127.0 - byte)[:, None, :]).reshape(k, n).astype(np.float32)
    by_word = np.ascontiguousarray(scaled.reshape(k // 512, 128, 4, n).transpose(0, 1, 3, 2))
    if fmt == "e4m3":
        words = by_word.astype(ml_dtypes.float8_e4m3fn).view(np.uint8)
    else:
        c = by_word.astype(ml_dtypes.float4_e2m1fn).view(np.uint8) & 0xF
        words = (c[..., 0::2] | (c[..., 1::2] << 4)).reshape(k // 512, 128, 2 * n)
    return np.ascontiguousarray(words), np.ascontiguousarray(byte.astype(np.uint8).reshape(k // 512, 16, n))


def unpack_weight(words, scales, fmt):
    g, _, n = scales.shape
    words = np.ascontiguousarray(words).reshape(g, 128, n, -1)
    if fmt == "e4m3":
        vals = words.view(ml_dtypes.float8_e4m3fn).astype(np.float64)
    else:
        nib = np.empty((g, 128, n, 4), np.uint8)
        nib[..., 0::2] = words & 0xF
        nib[..., 1::2] = words >> 4
        vals = E2M1[nib]
    vals = vals * np.repeat(np.exp2(scales.astype(np.float64) - 127.0), 8, axis=1)[..., None]
    return vals.transpose(0, 1, 3, 2).reshape(g * 512, n)


def gelu(v):
    return 0.5 * v * (1.0 + np.tanh(np.sqrt(2.0 / np.pi) * (v + 0.044715 * v**3)))


K, H, T, S, T3, S2, P = 1024, 512, 4096, 1024, 2048, 1024, 512

def setup_inputs():
    n = np.random.standard_normal
    s = mx_kscale(K)[:, None]
    u = mx_kscale(H)[:, None]
    d = {}
    d["tab_words"], d["tab_scales"] = pack_weight(n((K, T)) * s, "e4m3")
    d["tab2_words"], d["tab2_scales"] = pack_weight(0.7 * n((H, T3)) / H ** 0.5 / u, "e4m3")
    d["offs"] = striped(np.random.permutation(T)[:S])
    d["offs2"] = striped(np.random.permutation(T3)[:S2])
    d["pos1"] = striped(np.random.permutation(S)[:P])
    d["pos2"] = striped(np.random.permutation(S)[:P])
    d["w1"] = (n((K, H)) / K ** 0.5 / s * u.T).astype(np.float32)
    d["w4_words"], d["w4_scales"] = pack_weight(0.7 * n((K, H)) / K ** 0.5 / s * u.T, "e2m1")
    d["soil"] = (n((H, S)) * u).astype(np.float32)
    d["prog"] = np.exp(0.4 * n(S2)).astype(np.float32)
    return d

def reference(tab_words, tab_scales, tab2_words, tab2_scales, offs, offs2, pos1, pos2,
              w1, w4_words, w4_scales, soil, prog):
    v = unpack_weight(tab_words, tab_scales, "e4m3")[:, unstriped(offs)]
    v2 = unpack_weight(tab2_words, tab2_scales, "e4m3")[:, unstriped(offs2)]
    w4 = unpack_weight(w4_words, w4_scales, "e2m1")
    fibre = mxq(f64(w1), 0, "e4m3").T @ v
    weave = w4.T @ v
    h = np.maximum(fibre, f64(soil)) + weave
    e = v2.T @ mxq(h, 0, "e4m3")
    warp = e[:, unstriped(pos1)]
    weft = e[:, unstriped(pos2)]
    return np.square(warp * f64(prog)[:, None] + weft)

from contextlib import ExitStack

import concourse.mybir as mybir

K, H, T, S, T3, S2, NP = 1024, 512, 4096, 1024, 2048, 1024, 512
FLOPS = 2 * (2 * K * H * S + H * S2 * S)

F32 = mybir.dt.float32
BF16 = mybir.dt.bfloat16
I32 = mybir.dt.int32
U32 = mybir.dt.uint32
U16 = mybir.dt.uint16
U8 = mybir.dt.uint8
FP8X4 = mybir.dt.float8_e4m3fn_x4
FP4X4 = mybir.dt.float4_e2m1fn_x4
ALU = mybir.AluOpType
ACT = mybir.ActivationFunctionType

P = 128
PACK = 4
BANK = 512
PIECE = 256


def tile_list_linen_wear_scores_kernel(
    tc, tab_words, tab_scales, tab2_words, tab2_scales, offs, offs2, pos1, pos2,
    w1, w4_words, w4_scales, soil, prog, out,
):
    nc = tc.nc
    with ExitStack() as ctx:
        lists = ctx.enter_context(tc.tile_pool(name="lists", bufs=1))
        keep = ctx.enter_context(tc.tile_pool(name="keep", bufs=1))
        ring = ctx.enter_context(tc.tile_pool(name="ring", bufs=1))
        psum = ctx.enter_context(tc.psum_pool(name="psum", bufs=4))

        def kept(shape, dtype, name, tag=None):
            return keep.tile(shape, dtype, name=name, tag=tag or name, align_bytes=64)

        idx = lists.tile([P, S // 16], U16, name="idx")
        nc.sync.dma_start(idx[:], offs)
        v_scale_rows = kept([P, T], U8, "v_scale_rows", tag="slot_a")
        nc.sync.dma_start(
            v_scale_rows[0:32, :].bitcast(I32),
            tab_scales.rearrange("a q t -> (a q) t").bitcast(I32),
        )
        idx2 = lists.tile([P, S2 // 16], U16, name="idx2")
        nc.sync.dma_start(idx2[:], offs2)
        warp_list = lists.tile([P, NP // 16], U16, name="warp_list")
        nc.sync.dma_start(warp_list[:], pos1)
        weft_list = lists.tile([P, NP // 16], U16, name="weft_list")
        nc.sync.dma_start(weft_list[:], pos2)

        def load_words(words, width, name, tag):
            window = kept([P, width], U32, name, tag=tag)
            nc.sync.dma_start(window[:].bitcast(I32), words.rearrange("p t i -> p (t i)").bitcast(I32))
            return window

        v_window0 = load_words(tab_words[0], T, "v_window0", "slot_c")
        w4_raw = kept([P, 2, 2 * H], U8, "w4_raw", tag="slot_d")
        nc.sync.dma_start(w4_raw[:].bitcast(I32), w4_words.rearrange("a p c -> p a c").bitcast(I32))

        v2_scale_rows = kept([P, T3], U8, "v2_scale_rows", tag="slot_b")
        nc.vector.memset(v2_scale_rows[:].bitcast(I32), 0)
        nc.scalar.dma_start(v2_scale_rows[0:16, :].bitcast(I32), tab2_scales[0].bitcast(I32))
        w4_scale_raw = kept([P, 2, H], U8, "w4_scale_raw")
        nc.vector.memset(w4_scale_raw[:].bitcast(I32), 0)
        for q in range(4):
            nc.gpsimd.dma_start(
                w4_scale_raw[32 * q : 32 * q + 4, :, :].bitcast(I32),
                w4_scales[:, 4 * q : 4 * q + 4, :].rearrange("a r c -> r a c").bitcast(I32),
            )
        nc.vector.memset(v_scale_rows[32:64, :].bitcast(I32), 0)
        nc.vector.memset(v_scale_rows[64:128, :].bitcast(I32), 0)
        v_scales = [kept([P, S], U8, "v_scales%d" % a) for a in range(2)]
        v2_scales = kept([P, S2], U8, "v2_scales")
        for plane in v_scales + [v2_scales]:
            nc.vector.memset(plane[:].bitcast(I32), 0)

        v_scale_picked = kept([P, S], U8, "v_scale_picked")
        nc.vector.tensor_copy(v_scale_picked[:], v_scale_rows[:].indirect(idx[:]))
        v_window1 = load_words(tab_words[1], T, "v_window1", "slot_a")

        def place_rows(queue, plane, picked, first):
            for q in range(4):
                queue.dma_start(
                    plane[32 * q : 32 * q + 4, :].bitcast(I32),
                    picked[first + 4 * q : first + 4 * q + 4, :].bitcast(I32),
                )

        place_rows(nc.scalar, v_scales[0], v_scale_picked, 0)
        place_rows(nc.gpsimd, v_scales[1], v_scale_picked, 16)
        v2_scale_picked = kept([P, S2], U8, "v2_scale_picked")
        nc.vector.tensor_copy(v2_scale_picked[:], v2_scale_rows[:].indirect(idx2[:]))
        place_rows(nc.gpsimd, v2_scales, v2_scale_picked, 0)

        def load_w1(a, tag):
            raw = kept([P, PACK, H], F32, "w1_raw%d" % a, tag=tag)
            nc.sync.dma_start(raw[:], w1[512 * a : 512 * (a + 1), :].rearrange("(p j) c -> p j c", j=PACK))
            return raw

        w1_raw0 = load_w1(0, "slot_b")
        v_codes = [kept([P, S], U32, "v_codes%d" % a) for a in range(2)]
        nc.vector.tensor_copy(v_codes[0][:], v_window0[:].indirect(idx[:]))
        w1_raw1 = load_w1(1, "slot_c")

        w4_codes = kept([P, 2, 2 * H], U8, "w4_codes")
        nc.vector.tensor_copy(
            w4_codes[:].bitcast(U16).rearrange("p a (t m) -> p a m t", t=PACK),
            w4_raw[:].bitcast(U16).rearrange("p a (m t) -> p a m t", t=PACK),
        )
        w4_planes = kept([P, 2, H], U8, "w4_planes")
        nc.vector.tensor_copy(
            w4_planes[:].rearrange("p a (t m) -> p a m t", t=PACK),
            w4_scale_raw[:].rearrange("p a (m t) -> p a m t", t=PACK),
        )
        soil_rows = soil.rearrange("(p t) j -> p t j", t=PACK)
        soil_a = kept([P, 2, BANK], F32, "soil_a", tag="slot_d")
        nc.sync.dma_start(soil_a[:], soil_rows[:, 0:2, 0:BANK])
        nc.vector.tensor_copy(v_codes[1][:], v_window1[:].indirect(idx[:]))
        soil_b = kept([P, 2, BANK], F32, "soil_b", tag="slot_a")
        nc.sync.dma_start(soil_b[:], soil_rows[:, 2:4, 0:BANK])

        w1_codes = [[kept([P, 2 * P], U32, "w1_codes%d%d" % (a, u)) for u in range(2)] for a in range(2)]
        w1_planes = [[kept([P, 2 * P], U8, "w1_planes%d%d" % (a, u)) for u in range(2)] for a in range(2)]
        w1_grouped = [[kept([P, 2, P, PACK], BF16, "w1_grouped%d%d" % (a, u)) for u in range(2)] for a in range(2)]

        def w1_views(raw, a, u):
            dst = w1_grouped[a][u][:].rearrange("p t m j -> p m j t")
            src = raw[:].rearrange("p j (m t) -> p m j t", t=PACK)[:, :, :, 2 * u : 2 * u + 2]
            return dst, src

        def quantize_w1(a, u):
            nc.vector.quantize_mx(
                out=w1_codes[a][u][:].bitcast(FP8X4),
                scales=w1_planes[a][u][:],
                in_=w1_grouped[a][u][:].rearrange("p t m j -> p (t m j)"),
            )

        for u in range(2):
            dst, src = w1_views(w1_raw0, 0, u)
            nc.scalar.activation(dst, src, ACT.Copy)
        for u in range(2):
            quantize_w1(0, u)
        soil_c = kept([P, PACK, BANK], F32, "soil_c", tag="slot_b")
        nc.sync.dma_start(soil_c[:], soil_rows[:, :, BANK:S])
        dst, src = w1_views(w1_raw1, 1, 0)
        nc.vector.tensor_copy(dst, src)
        dst, src = w1_views(w1_raw1, 1, 1)
        nc.scalar.activation(dst, src, ACT.Copy)
        for u in range(2):
            quantize_w1(1, u)
        v2_window = load_words(tab2_words[0], T3, "v2_window", "slot_c")
        prog_cols = kept([P, S2 // P], F32, "prog_cols", tag="w1_grouped11")
        with nc.allow_non_contiguous_dma(reason="one factor a partition"):
            nc.sync.dma_start(prog_cols[:], prog.rearrange("(i p) -> p i", p=P))

        def soil_slice(half, t):
            if half == 1:
                return soil_c[:, t, :]
            return (soil_a, soil_b)[t // 2][:, t % 2, :]

        def fibre_pass(bank, half, t, a):
            cols = slice(BANK * half, BANK * (half + 1))
            wcols = slice(P * (t % 2), P * (t % 2 + 1))
            nc.tensor.matmul_mx(
                out=bank[:],
                lhsT=w1_codes[a][t // 2][:, wcols].bitcast(FP8X4),
                lhsT_scale=w1_planes[a][t // 2][:, wcols],
                rhs=v_codes[a][:, cols].bitcast(FP8X4),
                rhs_scale=v_scales[a][:, cols],
                start=(a == 0),
                stop=(a == 1),
            )

        def weave_pass(bank, half, t, a):
            cols = slice(BANK * half, BANK * (half + 1))
            nc.tensor.matmul_mx(
                out=bank[:],
                lhsT=w4_codes[:, a, 2 * P * t : 2 * P * (t + 1)].bitcast(FP4X4),
                lhsT_scale=w4_planes[:, a, P * t : P * (t + 1)],
                rhs=v_codes[a][:, cols].bitcast(FP8X4),
                rhs_scale=v_scales[a][:, cols],
                start=(a == 0),
                stop=(a == 1),
            )

        def new_bank(tag):
            return psum.tile([P, BANK], F32, name=tag, tag=tag)

        h_codes = kept([P, S], U32, "h_codes")
        h_planes = kept([P, S], U8, "h_planes")
        v2_codes = [kept([P, PIECE], U32, "v2_codes%d" % g) for g in range(S2 // PIECE)]

        def larger(bank, half, t):
            big = ring.tile([P, BANK], F32, name="big", tag="big", bufs=5)
            nc.vector.tensor_tensor(big[:], bank[:], soil_slice(half, t), ALU.max)
            return big

        def interleave(rows, width, name):
            woven = kept([P, width, PACK], BF16, name)
            nc.scalar.copy(
                woven[:].rearrange("p (c i) t -> p c t i", i=4),
                rows[:].rearrange("p t (c i) -> p c t i", i=4),
            )
            return woven

        def quantize_h(woven, first, width):
            nc.vector.quantize_mx(
                out=h_codes[:, first : first + width].bitcast(FP8X4),
                scales=h_planes[:, first : first + width],
                in_=woven[:].rearrange("p j t -> p (j t)"),
            )

        def gather_v2(g):
            cols = PIECE // 16
            nc.vector.tensor_copy(v2_codes[g][:], v2_window[:].indirect(idx2[:, g * cols : (g + 1) * cols]))

        scores = {}

        def score_half(i, half):
            if half == 0:
                scores[i] = ring.tile([P, S], F32, name="scores", tag="scores", bufs=6)
            bank = new_bank(("fibre", "weave")[half])
            cols = slice(BANK * half, BANK * (half + 1))
            g, first = divmod(P * i, PIECE)
            nc.tensor.matmul_mx(
                out=bank[:],
                lhsT=v2_codes[g][:, first : first + P].bitcast(FP8X4),
                lhsT_scale=v2_scales[:, P * i : P * (i + 1)],
                rhs=h_codes[:, cols].bitcast(FP8X4),
                rhs_scale=h_planes[:, cols],
                start=True,
                stop=True,
            )
            nc.scalar.copy(scores[i][:, cols], bank[:])

        fibre0 = [new_bank("fibre") for t in range(PACK)]
        weave0 = [new_bank("weave") for t in range(PACK)]
        for t in range(PACK):
            for a in range(2):
                weave_pass(weave0[t], 0, t, a)
        for a in range(2):
            for t in range(PACK):
                fibre_pass(fibre0[t], 0, t, a)

        rows0 = kept([P, PACK, BANK], BF16, "rows0")
        fibre1 = []
        weave1 = []
        big0 = []
        for step in range(PACK + 1):
            if step < PACK:
                big0.append(larger(fibre0[step], 0, step))
                fibre1.append(new_bank("fibre"))
                for a in range(2):
                    fibre_pass(fibre1[step], 1, step, a)
            if step > 0:
                t = step - 1
                nc.vector.tensor_tensor(rows0[:, t, :], weave0[t][:], big0[t][:], ALU.add)
                weave1.append(new_bank("weave"))
                for a in range(2):
                    weave_pass(weave1[t], 1, t, a)
        woven0 = interleave(rows0, BANK, "woven0")
        big1 = [larger(fibre1[t], 1, t) for t in range(PACK)]
        quantize_h(woven0, 0, BANK)
        gather_v2(0)
        for i in range(2):
            score_half(i, 0)
        woven1 = []
        for c in range(2):
            cols = slice(PIECE * c, PIECE * (c + 1))
            rows1 = kept([P, PACK, PIECE], BF16, "rows1%d" % c)
            for t in range(PACK):
                nc.vector.tensor_tensor(rows1[:, t, :], weave1[t][:, cols], big1[t][:, cols], ALU.add)
            woven1.append(interleave(rows1, PIECE, "woven1%d" % c))
        quantize_h(woven1[0], BANK, PIECE)
        quantize_h(woven1[1], BANK + PIECE, PIECE)
        score_half(0, 1)
        for g in range(1, S2 // PIECE):
            gather_v2(g)
        score_half(1, 1)

        tiles = S2 // P
        weighted = {}
        for step in range(tiles + 1):
            if step < tiles:
                warp = ring.tile([P, NP], F32, name="warp", tag="warp", bufs=3)
                nc.vector.tensor_copy(warp[:], scores[step][:].indirect(warp_list[:]))
                weighted[step] = ring.tile([P, NP], F32, name="weighted", tag="weighted", bufs=3)
                nc.scalar.activation(weighted[step][:], warp[:], ACT.Copy, scale=prog_cols[:, step : step + 1])
            if step + 2 < tiles:
                for half in range(2):
                    score_half(step + 2, half)
            if step > 0:
                i = step - 1
                total = ring.tile([P, NP], F32, name="total", tag="total", bufs=3)
                nc.vector.tensor_tensor(total[:], scores[i][:].indirect(weft_list[:]), weighted[i][:], ALU.add)
                result = ring.tile([P, NP], F32, name="result", tag="result", bufs=3)
                nc.scalar.activation(result[:], total[:], ACT.Square)
                nc.sync.dma_start(out[P * i : P * (i + 1), :], result[:])
